import numpy as np
import ml_dtypes


def mxq(x, axis, fmt="e4m3"):
    dtype, down = {"e4m3": (ml_dtypes.float8_e4m3fn, 7), "e5m2": (ml_dtypes.float8_e5m2, 14)}[fmt]
    v = np.moveaxis(np.asarray(x, np.float32).astype(ml_dtypes.bfloat16).astype(np.float64), axis, -1)
    blocks = v.reshape(v.shape[:-1] + (-1, 32))
    amax = np.abs(blocks).max(-1, keepdims=True)
    byte = np.maximum(np.where(amax > 0, np.frexp(amax)[1] - 1 + 127, 0) - down, 1)
    scale = np.exp2(byte - 127.0)
    codes = (blocks / scale).astype(np.float32).astype(dtype).astype(np.float64)
    return np.moveaxis((codes * scale).reshape(v.shape), -1, axis)


WIDE = False


def mx_kscale(k):
    if not WIDE:
        return np.ones(k)
    levels = np.array([10, -10, 5, -5, 0])
    if k % 512:
        return np.exp2(np.random.permutation(np.resize(levels, k // 32))).repeat(32)
    a = np.empty((k // 512, 16))
    for p in range(k // 512):
        a[p, :8] = np.random.permutation(np.resize(levels, 8))
        for g in range(8):
            far = levels[np.abs(levels - a[p, g]) >= 10]
            a[p, g + 8] = far[np.random.randint(len(far))]
    return np.exp2(a.ravel()).repeat(32)


def f64(x):
    return np.asarray(x).astype(np.float64)


def striped(idx):
    return np.tile(idx.reshape(-1, 16).T, (8, 1)).astype(np.uint16)


def unstriped(offs):
    return offs[:16].T.reshape(-1).astype(np.int64)


def silu(v):
    return v / (1.0 + np.exp(-np.maximum(v, -700.0)))


K, T, E, C, N = 1024, 512, 16, 128, 256
TOP = 4


def by_expert(wq, xq):
    return np.concatenate([wq[e].T @ xq[:, e * C:(e + 1) * C] for e in range(E)], axis=1)


def setup_inputs():
    n = np.random.standard_normal
    s = mx_kscale(K)[:, None]
    deal = np.repeat(np.arange(E), C).reshape(TOP, T)[:, np.random.permutation(T)]
    deal = np.take_along_axis(deal, np.argsort(np.random.rand(TOP, T), axis=0), axis=0)
    for _ in range(8):
        s_, t_ = np.random.permutation(T).reshape(2, -1); r = np.random.randint(TOP, size=T // 2); x, y = deal[r, s_].copy(), deal[r, t_].copy()
        ok = ~((deal[:, s_] == y).any(0) | (deal[:, t_] == x).any(0)); deal[r[ok], s_[ok]] = y[ok]; deal[r[ok], t_[ok]] = x[ok]
    order = np.lexsort((np.random.rand(TOP * T), deal.reshape(-1)))
    slot_token = order % T; pos = np.empty(TOP * T, np.int64); pos[order] = np.arange(TOP * T); pos = pos.reshape(TOP, T)
    g = np.random.uniform(0.5, 1.5, (TOP, T)); g = g / g.sum(0)
    return {
        "xT": (n((K, T)) * s).astype(np.float32),
        "w": (n((E, K, N)) / np.sqrt(K) / s[None]).astype(np.float32),
        "b": (0.3 * n((N, E))).astype(np.float32),
        "gate": np.stack([np.tile(r, (N, 1)) for r in g]).astype(np.float32),
        "offs": striped(slot_token),
        "pos1": striped(pos[0]),
        "pos2": striped(pos[1]),
        "pos3": striped(pos[2]),
        "pos4": striped(pos[3]),
    }


def reference(xT, w, b, gate, offs, pos1, pos2, pos3, pos4):
    idx = unstriped(offs)
    xq = mxq(f64(xT)[:, idx], 0, "e4m3")
    y = by_expert(mxq(f64(w), 1, "e4m3"), xq)
    y = silu(y + np.repeat(f64(b), C, axis=1))
    return sum(f64(gate[r]) * y[:, unstriped(p)] for r, p in enumerate((pos1, pos2, pos3, pos4)))

@@ -1,0 +1,163 @@
+from contextlib import ExitStack
+
+import concourse.mybir as mybir
+
+K, T, E, C, N = 1024, 512, 16, 128, 256
+TOP = 4
+FLOPS = 2 * TOP * T * K * N
+
+F32 = mybir.dt.float32
+BF16 = mybir.dt.bfloat16
+U32 = mybir.dt.uint32
+U16 = mybir.dt.uint16
+U8 = mybir.dt.uint8
+FP8X4 = mybir.dt.float8_e4m3fn_x4
+SILU = mybir.ActivationFunctionType.Silu
+MULT = mybir.AluOpType.mult
+ADD = mybir.AluOpType.add
+
+P = 128
+PACK = 4
+PASSES = K // (P * PACK)
+HALVES = N // P
+SLOTS = E * C
+PIECES = (2, 3, 3, 3, 3, 2)
+W_SCALAR = 176
+X_SCALAR = 192
+
+
+def tile_moe_tk_lin_silu_kernel(tc, xT, w, b, gate, offs, pos1, pos2, pos3, pos4, out):
+    nc = tc.nc
+    with ExitStack() as ctx:
+        keep = ctx.enter_context(tc.tile_pool(name="keep", bufs=1))
+        raws = ctx.enter_context(tc.tile_pool(name="raws", bufs=7))
+        work = ctx.enter_context(tc.tile_pool(name="work", bufs=4))
+        slots = ctx.enter_context(tc.tile_pool(name="slots", bufs=2))
+        psum = ctx.enter_context(tc.psum_pool(name="psum", bufs=4))
+
+        offs_sb = keep.tile([P, SLOTS // 16], U16, name="offs_sb")
+        pos_sb = [keep.tile([P, T // 16], U16, name="pos_sb%d" % r) for r in range(TOP)]
+        bias = keep.tile([P, HALVES, E], F32, name="bias")
+        warm = keep.tile([P, 1], F32, name="warm")
+        warmed = keep.tile([P, 1], F32, name="warmed")
+        x_raw = [keep.tile([P, PACK * T], F32, name="x_raw%d" % a) for a in range(PASSES)]
+        x_grouped = [keep.tile([P, T, PACK], BF16, name="x_grouped%d" % a, align_bytes=64) for a in range(PASSES)]
+        x_codes = [keep.tile([P, T], U32, name="x_codes%d" % a, align_bytes=64) for a in range(PASSES)]
+        x_scales = keep.tile([P, T], U8, name="x_scales", align_bytes=64)
+        y = [keep.tile([P, SLOTS], F32, name="y%d" % h) for h in range(HALVES)]
+        gates = [keep.tile([P, TOP, T], F32, name="gates%d" % h) for h in range(HALVES)]
+        prod = [keep.tile([P, TOP, T], F32, name="prod%d" % h) for h in range(HALVES)]
+        res = [keep.tile([P, T], F32, name="res%d" % h) for h in range(HALVES)]
+
+        nc.gpsimd.memset(warm[:], 0.0)
+        nc.gpsimd.memset(x_scales[:], 0)
+        nc.scalar.activation(warmed[:], warm[:], SILU)
+
+        for a in range(PASSES):
+            nc.sync.dma_start(x_raw[a][:], xT[a * 512 : (a + 1) * 512, :].rearrange("(p j) t -> p (j t)", j=PACK))
+        nc.sync.dma_start(offs_sb[:], offs)
+
+        w_raw, w_grouped, w_codes, w_scales = {}, {}, {}, {}
+
+        def load(e):
+            w_raw[e] = raws.tile([P, PASSES, PACK * N], F32, name="w_raw")
+            nc.sync.dma_start(w_raw[e][:], w[e].rearrange("(a p j) n -> p a (j n)", a=PASSES, j=PACK))
+
+        def interleave(e):
+            w_grouped[e] = work.tile([P, PASSES, N, PACK], BF16, name="w_grouped", align_bytes=64)
+            view = w_raw[e][:].rearrange("p a (j n) -> p a n j", j=PACK)
+            nc.scalar.copy(w_grouped[e][:, :, 0:W_SCALAR, :], view[:, :, 0:W_SCALAR, :])
+            nc.vector.tensor_copy(w_grouped[e][:, :, W_SCALAR:N, :], view[:, :, W_SCALAR:N, :])
+
+        def quantise(e):
+            w_codes[e] = work.tile([P, PASSES * N], U32, name="w_codes", align_bytes=64)
+            w_scales[e] = work.tile([P, PASSES * N], U8, name="w_scales", align_bytes=64)
+            nc.vector.quantize_mx(
+                out=w_codes[e][:].bitcast(FP8X4),
+                scales=w_scales[e][:],
+                in_=w_grouped[e][:].rearrange("p a n j -> p (a n j)"),
+            )
+
+        def multiply(e):
+            for h in range(HALVES):
+                acc = psum.tile([P, C], F32, name="acc%d" % h)
+                for a in range(PASSES):
+                    cols = slice(a * N + h * P, a * N + (h + 1) * P)
+                    codes, here = place[(e, a)]
+                    scales, there = place[(e, PASSES)]
+                    nc.tensor.matmul_mx(
+                        out=acc[:],
+                        lhsT=w_codes[e][:, cols].bitcast(FP8X4),
+                        lhsT_scale=w_scales[e][:, cols],
+                        rhs=codes[:, here].bitcast(FP8X4),
+                        rhs_scale=scales[4 * a : P, there],
+                        start=(a == 0),
+                        stop=(a == PASSES - 1),
+                    )
+                nc.scalar.activation(y[h][:, e * C : (e + 1) * C], acc[:], SILU, bias=bias[:, h, e : e + 1])
+
+        first = [sum(PIECES[:g]) for g in range(len(PIECES))]
+        todo = [(g, k) for g in range(len(PIECES)) for k in range(PASSES + 1)]
+        place = {}
+
+        def gather(count):
+            for i in range(count):
+                if todo:
+                    g, k = todo.pop(0)
+                    n = PIECES[g] * C
+                    c0 = first[g] * C // 16
+                    if k < PASSES:
+                        src = x_codes[k]
+                        dst = slots.tile([P, 3 * C], U32, name="s_codes%d" % k, align_bytes=64)
+                    else:
+                        src = x_scales
+                        dst = slots.tile([P, 3 * C], U8, name="s_scales", align_bytes=64)
+                    nc.vector.tensor_copy(dst[:, 0:n], src[:].indirect(offs_sb[:, c0 : c0 + n // 16]))
+                    for i in range(PIECES[g]):
+                        place[(first[g] + i, k)] = (dst, slice(i * C, (i + 1) * C))
+
+        for a in range(PASSES):
+            view = x_raw[a][:].rearrange("p (j t) -> p t j", j=PACK)
+            nc.scalar.copy(x_grouped[a][:, 0:X_SCALAR, :], view[:, 0:X_SCALAR, :])
+            nc.vector.tensor_copy(x_grouped[a][:, X_SCALAR:T, :], view[:, X_SCALAR:T, :])
+        for a in range(PASSES):
+            nc.vector.quantize_mx(
+                out=x_codes[a][:].bitcast(FP8X4),
+                scales=x_scales[4 * a : P, :],
+                in_=x_grouped[a][:].rearrange("p t j -> p (t j)"),
+            )
+
+        for step in range(E + 2):
+            if step < E:
+                load(step)
+            if step == 0:
+                nc.sync.dma_start(bias[:], b.rearrange("(h p) e -> p h e", p=P))
+            if step == 6:
+                for r, pos in enumerate((pos1, pos2, pos3, pos4)):
+                    nc.sync.dma_start(pos_sb[r][:], pos)
+            if step < E:
+                interleave(step)
+            gather(3 if step == 0 else 1)
+            if 1 <= step <= E:
+                quantise(step - 1)
+            if step >= 2:
+                multiply(step - 2)
+        for h in range(HALVES):
+            for r in range(0, TOP, 2):
+                nc.sync.dma_start(gates[h][:, r : r + 2, :], gate[r : r + 2, h * P : (h + 1) * P, :].rearrange("r p t -> p r t"))
+
+        for h in range(HALVES):
+            rows = slice(h * P, (h + 1) * P)
+            for r in range(TOP - 1):
+                nc.vector.tensor_tensor(prod[h][:, r, :], y[h][:].indirect(pos_sb[r][:]), gates[h][:, r, :], MULT)
+            nc.vector.tensor_tensor(prod[h][:, 0, :], prod[h][:, 0, :], prod[h][:, 1, :], ADD)
+            r = TOP - 1
+            halves = ((0, 256), (256, 512))
+            t0, t1 = halves[0]
+            nc.vector.tensor_tensor(prod[h][:, r, t0:t1], y[h][:].indirect(pos_sb[r][:, t0 // 16 : t1 // 16]), gates[h][:, r, t0:t1], MULT)
+            nc.vector.tensor_tensor(prod[h][:, 0, :], prod[h][:, 0, :], prod[h][:, 2, :], ADD)
+            t0, t1 = halves[1]
+            nc.vector.tensor_tensor(prod[h][:, r, t0:t1], y[h][:].indirect(pos_sb[r][:, t0 // 16 : t1 // 16]), gates[h][:, r, t0:t1], MULT)
+            for t0, t1 in halves:
+                nc.vector.tensor_tensor(res[h][:, t0:t1], prod[h][:, 0, t0:t1], prod[h][:, r, t0:t1], ADD)
+                nc.sync.dma_start(out[rows, t0:t1], res[h][:, t0:t1])

@@ -22,15 +22,22 @@ PASSES = K // (P * PACK)
 HALVES = N // P
 SLOTS = E * C
 PIECES = (2, 3, 3, 3, 3, 2)
-W_SCALAR = 176
+LATE = 3
+WHOLE = E - LATE
+VECTOR_EXPERTS = (2, 6, 10)
+HALF_SCALAR = 80
 X_SCALAR = 192
+RUNS = (4, 4, 4, 1, 2, 1, 2, 1)
+RUN = 4
 
 
 def tile_moe_tk_lin_silu_kernel(tc, xT, w, b, gate, offs, pos1, pos2, pos3, pos4, out):
     nc = tc.nc
     with ExitStack() as ctx:
         keep = ctx.enter_context(tc.tile_pool(name="keep", bufs=1))
-        raws = ctx.enter_context(tc.tile_pool(name="raws", bufs=7))
+        raws = ctx.enter_context(tc.tile_pool(name="raws", bufs=6))
+        late = ctx.enter_context(tc.tile_pool(name="late", bufs=6))
+        wide = ctx.enter_context(tc.tile_pool(name="wide", bufs=6))
         work = ctx.enter_context(tc.tile_pool(name="work", bufs=4))
         slots = ctx.enter_context(tc.tile_pool(name="slots", bufs=2))
         psum = ctx.enter_context(tc.psum_pool(name="psum", bufs=4))
@@ -56,45 +63,18 @@ def tile_moe_tk_lin_silu_kernel(tc, xT, w, b, gate, offs, pos1, pos2, pos3, pos4
         for a in range(PASSES):
             nc.sync.dma_start(x_raw[a][:], xT[a * 512 : (a + 1) * 512, :].rearrange("(p j) t -> p (j t)", j=PACK))
         nc.sync.dma_start(offs_sb[:], offs)
-
-        w_raw, w_grouped, w_codes, w_scales = {}, {}, {}, {}
-
-        def load(e):
-            w_raw[e] = raws.tile([P, PASSES, PACK * N], F32, name="w_raw")
-            nc.sync.dma_start(w_raw[e][:], w[e].rearrange("(a p j) n -> p a (j n)", a=PASSES, j=PACK))
-
-        def interleave(e):
-            w_grouped[e] = work.tile([P, PASSES, N, PACK], BF16, name="w_grouped", align_bytes=64)
-            view = w_raw[e][:].rearrange("p a (j n) -> p a n j", j=PACK)
-            nc.scalar.copy(w_grouped[e][:, :, 0:W_SCALAR, :], view[:, :, 0:W_SCALAR, :])
-            nc.vector.tensor_copy(w_grouped[e][:, :, W_SCALAR:N, :], view[:, :, W_SCALAR:N, :])
-
-        def quantise(e):
-            w_codes[e] = work.tile([P, PASSES * N], U32, name="w_codes", align_bytes=64)
-            w_scales[e] = work.tile([P, PASSES * N], U8, name="w_scales", align_bytes=64)
+        for a in range(PASSES):
+            dest = x_grouped[a][:].rearrange("p (c i) j -> p c j i", i=RUN)
+            view = x_raw[a][:].rearrange("p (j c i) -> p c j i", j=PACK, i=RUN)
+            cut = X_SCALAR // RUN
+            nc.scalar.copy(dest[:, 0:cut], view[:, 0:cut])
+            nc.vector.tensor_copy(dest[:, cut:], view[:, cut:])
+        for a in range(PASSES):
             nc.vector.quantize_mx(
-                out=w_codes[e][:].bitcast(FP8X4),
-                scales=w_scales[e][:],
-                in_=w_grouped[e][:].rearrange("p a n j -> p (a n j)"),
+                out=x_codes[a][:].bitcast(FP8X4),
+                scales=x_scales[4 * a : P, :],
+                in_=x_grouped[a][:].rearrange("p t j -> p (t j)"),
             )
-
-        def multiply(e):
-            for h in range(HALVES):
-                acc = psum.tile([P, C], F32, name="acc%d" % h)
-                for a in range(PASSES):
-                    cols = slice(a * N + h * P, a * N + (h + 1) * P)
-                    codes, here = place[(e, a)]
-                    scales, there = place[(e, PASSES)]
-                    nc.tensor.matmul_mx(
-                        out=acc[:],
-                        lhsT=w_codes[e][:, cols].bitcast(FP8X4),
-                        lhsT_scale=w_scales[e][:, cols],
-                        rhs=codes[:, here].bitcast(FP8X4),
-                        rhs_scale=scales[4 * a : P, there],
-                        start=(a == 0),
-                        stop=(a == PASSES - 1),
-                    )
-                nc.scalar.activation(y[h][:, e * C : (e + 1) * C], acc[:], SILU, bias=bias[:, h, e : e + 1])
 
         first = [sum(PIECES[:g]) for g in range(len(PIECES))]
         todo = [(g, k) for g in range(len(PIECES)) for k in range(PASSES + 1)]
@@ -116,48 +96,155 @@ def tile_moe_tk_lin_silu_kernel(tc, xT, w, b, gate, offs, pos1, pos2, pos3, pos4
                     for i in range(PIECES[g]):
                         place[(first[g] + i, k)] = (dst, slice(i * C, (i + 1) * C))
 
-        for a in range(PASSES):
-            view = x_raw[a][:].rearrange("p (j t) -> p t j", j=PACK)
-            nc.scalar.copy(x_grouped[a][:, 0:X_SCALAR, :], view[:, 0:X_SCALAR, :])
-            nc.vector.tensor_copy(x_grouped[a][:, X_SCALAR:T, :], view[:, X_SCALAR:T, :])
-        for a in range(PASSES):
+        parcels = [(e, None) for e in range(WHOLE)]
+        for h in range(HALVES):
+            parcels.extend([(e, h) for e in range(WHOLE, E)])
+        raw, grouped, weights, banks = {}, {}, {}, {}
+        ends = [sum(RUNS[: i + 1]) - 1 for i in range(len(RUNS))]
+
+        def load(u):
+            e, h = parcels[u]
+            if h is None:
+                raw[u] = raws.tile([P, PASSES, PACK, N], F32, name="w_raw")
+                src = w[e].rearrange("(a p j) n -> p a (j n)", a=PASSES, j=PACK)
+                nc.sync.dma_start(raw[u][:].rearrange("p a j n -> p a (j n)"), src)
+            else:
+                raw[u] = late.tile([P, PASSES, PACK, P], F32, name="half_raw")
+                for a in range(PASSES):
+                    src = w[e, a * 512 : (a + 1) * 512, h * P : (h + 1) * P].rearrange("(p j) n -> p j n", j=PACK)
+                    nc.sync.dma_start(raw[u][:, a], src)
+
+        def spread(u):
+            e, h = parcels[u]
+            view = raw[u][:].rearrange("p a j (c i) -> p a c j i", i=RUN)
+            if h is None:
+                grouped[u] = wide.tile([P, PASSES, N, PACK], BF16, name="w_grouped", align_bytes=64)
+            else:
+                grouped[u] = late.tile([P, PASSES, P, PACK], BF16, name="half_grouped", align_bytes=64)
+            dest = grouped[u][:].rearrange("p a (c i) j -> p a c j i", i=RUN)
+            if h is None and e in VECTOR_EXPERTS:
+                nc.vector.tensor_copy(dest, view)
+            elif h == 0:
+                cut = HALF_SCALAR // RUN
+                nc.scalar.copy(dest[:, :, 0:cut], view[:, :, 0:cut])
+                nc.vector.tensor_copy(dest[:, :, cut:], view[:, :, cut:])
+            else:
+                nc.scalar.copy(dest, view)
+
+        def quantise(u):
+            e, h = parcels[u]
+            n = PASSES * (N if h is None else P)
+            pool, tag = (work, "w") if h is None else (late, "half")
+            codes = pool.tile([P, n], U32, name=tag + "_codes", align_bytes=64)
+            scales = pool.tile([P, n], U8, name=tag + "_scales", align_bytes=64)
+            weights[u] = (codes, scales)
             nc.vector.quantize_mx(
-                out=x_codes[a][:].bitcast(FP8X4),
-                scales=x_scales[4 * a : P, :],
-                in_=x_grouped[a][:].rearrange("p t j -> p (t j)"),
+                out=codes[:].bitcast(FP8X4),
+                scales=scales[:],
+                in_=grouped[u][:].rearrange("p a n j -> p (a n j)"),
             )
 
-        for step in range(E + 2):
-            if step < E:
-                load(step)
-            if step == 0:
-                nc.sync.dma_start(bias[:], b.rearrange("(h p) e -> p h e", p=P))
-            if step == 6:
-                for r, pos in enumerate((pos1, pos2, pos3, pos4)):
-                    nc.sync.dma_start(pos_sb[r][:], pos)
-            if step < E:
-                interleave(step)
-            gather(3 if step == 0 else 1)
-            if 1 <= step <= E:
-                quantise(step - 1)
-            if step >= 2:
-                multiply(step - 2)
-        for h in range(HALVES):
+        def multiply(u):
+            e, h = parcels[u]
+            run = len([end for end in ends if end < u])
+            u0 = ends[run] + 1 - RUNS[run]
+            halves = range(HALVES) if h is None else (h,)
+            if u == u0:
+                for q in halves:
+                    banks[(run, q)] = psum.tile([P, 4 * C], F32, name="acc%d" % q)
+            w_codes, w_scales = weights[u]
+            for q in halves:
+                acc = banks[(run, q)]
+                for a in range(PASSES):
+                    c0 = a * N + q * P if h is None else a * P
+                    codes, here = place[(e, a)]
+                    scales, there = place[(e, PASSES)]
+                    nc.tensor.matmul_mx(
+                        out=acc[:, (u - u0) * C : (u - u0 + 1) * C],
+                        lhsT=w_codes[:, c0 : c0 + P].bitcast(FP8X4),
+                        lhsT_scale=w_scales[:, c0 : c0 + P],
+                        rhs=codes[:, here].bitcast(FP8X4),
+                        rhs_scale=scales[4 * a : P, there],
+                        start=(a == 0),
+                        stop=(a == PASSES - 1),
+                    )
+            if u == ends[run]:
+                for q in halves:
+                    for v in range(u0, u + 1):
+                        f = parcels[v][0]
+                        nc.scalar.activation(
+                            y[q][:, f * C : (f + 1) * C],
+                            banks[(run, q)][:, (v - u0) * C : (v - u0 + 1) * C],
+                            SILU,
+                            bias=bias[:, q, f : f + 1],
+                        )
+
+        def load_gates(h):
             for r in range(0, TOP, 2):
                 nc.sync.dma_start(gates[h][:, r : r + 2, :], gate[r : r + 2, h * P : (h + 1) * P, :].rearrange("r p t -> p r t"))
 
-        for h in range(HALVES):
-            rows = slice(h * P, (h + 1) * P)
-            for r in range(TOP - 1):
-                nc.vector.tensor_tensor(prod[h][:, r, :], y[h][:].indirect(pos_sb[r][:]), gates[h][:, r, :], MULT)
-            nc.vector.tensor_tensor(prod[h][:, 0, :], prod[h][:, 0, :], prod[h][:, 1, :], ADD)
-            r = TOP - 1
-            halves = ((0, 256), (256, 512))
-            t0, t1 = halves[0]
-            nc.vector.tensor_tensor(prod[h][:, r, t0:t1], y[h][:].indirect(pos_sb[r][:, t0 // 16 : t1 // 16]), gates[h][:, r, t0:t1], MULT)
-            nc.vector.tensor_tensor(prod[h][:, 0, :], prod[h][:, 0, :], prod[h][:, 2, :], ADD)
-            t0, t1 = halves[1]
-            nc.vector.tensor_tensor(prod[h][:, r, t0:t1], y[h][:].indirect(pos_sb[r][:, t0 // 16 : t1 // 16]), gates[h][:, r, t0:t1], MULT)
-            for t0, t1 in halves:
-                nc.vector.tensor_tensor(res[h][:, t0:t1], prod[h][:, 0, t0:t1], prod[h][:, r, t0:t1], ADD)
-                nc.sync.dma_start(out[rows, t0:t1], res[h][:, t0:t1])
+        def combine(h, adds):
+            low, high = slice(0, T // 2), slice(T // 2, T)
+            part = prod[h]
+            last = TOP - 1
+
+            def pick(r):
+                nc.vector.tensor_tensor(part[:, r, :], y[h][:].indirect(pos_sb[r][:]), gates[h][:, r, :], MULT)
+
+            def pick_half(cols):
+                offsets = pos_sb[last][:, cols.start // 16 : cols.stop // 16]
+                nc.vector.tensor_tensor(part[:, last, cols], y[h][:].indirect(offsets), gates[h][:, last, cols], MULT)
+
+            def add(r):
+                nc.vector.tensor_tensor(part[:, 0, :], part[:, 0, :], part[:, r, :], ADD)
+
+            def finish(cols):
+                nc.vector.tensor_tensor(res[h][:, cols], part[:, 0, cols], part[:, last, cols], ADD)
+                nc.sync.dma_start(out[h * P : (h + 1) * P, cols], res[h][:, cols])
+
+            if h == 0:
+                if not adds:
+                    for r in range(TOP):
+                        pick(r)
+                else:
+                    add(1)
+                    add(2)
+                    finish(slice(0, T))
+            else:
+                for r in range(last):
+                    pick(r)
+                add(1)
+                pick_half(low)
+                add(2)
+                pick_half(high)
+                finish(low)
+                finish(high)
+
+        h1 = WHOLE + LATE
+        for step in range(h1 + 2):
+            if step < h1:
+                load(step)
+            if step == 0:
+                nc.sync.dma_start(bias[:], b.rearrange("(h p) e -> p h e", p=P))
+            if step >= 2:
+                multiply(step - 2)
+            if 1 <= step <= h1:
+                quantise(step - 1)
+            gather(3 if step == 0 else 1)
+            if step < h1:
+                spread(step)
+            if step == h1 - 1:
+                for r, pos in enumerate((pos1, pos2, pos3, pos4)):
+                    nc.sync.dma_start(pos_sb[r][:], pos)
+                load_gates(0)
+                for u in range(h1, len(parcels)):
+                    load(u)
+                load_gates(1)
+        for u in range(h1, len(parcels)):
+            spread(u)
+        combine(0, False)
+        for u in range(h1, len(parcels)):
+            quantise(u)
+            multiply(u)
+        combine(0, True)
+        combine(1, True)

from contextlib import ExitStack

import concourse.mybir as mybir

K, T, E, C, N = 1024, 512, 16, 128, 256
TOP = 4
FLOPS = 2 * TOP * T * K * N

F32 = mybir.dt.float32
BF16 = mybir.dt.bfloat16
U32 = mybir.dt.uint32
U16 = mybir.dt.uint16
U8 = mybir.dt.uint8
FP8X4 = mybir.dt.float8_e4m3fn_x4
SILU = mybir.ActivationFunctionType.Silu
MULT = mybir.AluOpType.mult
ADD = mybir.AluOpType.add

P = 128
PACK = 4
PASSES = K // (P * PACK)
HALVES = N // P
SLOTS = E * C
PIECES = (2, 3, 3, 3, 3, 2)
LATE = 3
WHOLE = E - LATE
VECTOR_EXPERTS = (2, 6, 10)
HALF_SCALAR = 80
X_SCALAR = 192
RUNS = (4, 4, 4, 1, 2, 1, 2, 1)
RUN = 4


def tile_moe_tk_lin_silu_kernel(tc, xT, w, b, gate, offs, pos1, pos2, pos3, pos4, out):
    nc = tc.nc
    with ExitStack() as ctx:
        keep = ctx.enter_context(tc.tile_pool(name="keep", bufs=1))
        raws = ctx.enter_context(tc.tile_pool(name="raws", bufs=6))
        late = ctx.enter_context(tc.tile_pool(name="late", bufs=6))
        wide = ctx.enter_context(tc.tile_pool(name="wide", bufs=6))
        work = ctx.enter_context(tc.tile_pool(name="work", bufs=4))
        slots = ctx.enter_context(tc.tile_pool(name="slots", bufs=2))
        psum = ctx.enter_context(tc.psum_pool(name="psum", bufs=4))

        offs_sb = keep.tile([P, SLOTS // 16], U16, name="offs_sb")
        pos_sb = [keep.tile([P, T // 16], U16, name="pos_sb%d" % r) for r in range(TOP)]
        bias = keep.tile([P, HALVES, E], F32, name="bias")
        warm = keep.tile([P, 1], F32, name="warm")
        warmed = keep.tile([P, 1], F32, name="warmed")
        x_raw = [keep.tile([P, PACK * T], F32, name="x_raw%d" % a) for a in range(PASSES)]
        x_grouped = [keep.tile([P, T, PACK], BF16, name="x_grouped%d" % a, align_bytes=64) for a in range(PASSES)]
        x_codes = [keep.tile([P, T], U32, name="x_codes%d" % a, align_bytes=64) for a in range(PASSES)]
        x_scales = keep.tile([P, T], U8, name="x_scales", align_bytes=64)
        y = [keep.tile([P, SLOTS], F32, name="y%d" % h) for h in range(HALVES)]
        gates = [keep.tile([P, TOP, T], F32, name="gates%d" % h) for h in range(HALVES)]
        prod = [keep.tile([P, TOP, T], F32, name="prod%d" % h) for h in range(HALVES)]
        res = [keep.tile([P, T], F32, name="res%d" % h) for h in range(HALVES)]

        nc.gpsimd.memset(warm[:], 0.0)
        nc.gpsimd.memset(x_scales[:], 0)
        nc.scalar.activation(warmed[:], warm[:], SILU)

        for a in range(PASSES):
            nc.sync.dma_start(x_raw[a][:], xT[a * 512 : (a + 1) * 512, :].rearrange("(p j) t -> p (j t)", j=PACK))
        nc.sync.dma_start(offs_sb[:], offs)
        for a in range(PASSES):
            dest = x_grouped[a][:].rearrange("p (c i) j -> p c j i", i=RUN)
            view = x_raw[a][:].rearrange("p (j c i) -> p c j i", j=PACK, i=RUN)
            cut = X_SCALAR // RUN
            nc.scalar.copy(dest[:, 0:cut], view[:, 0:cut])
            nc.vector.tensor_copy(dest[:, cut:], view[:, cut:])
        for a in range(PASSES):
            nc.vector.quantize_mx(
                out=x_codes[a][:].bitcast(FP8X4),
                scales=x_scales[4 * a : P, :],
                in_=x_grouped[a][:].rearrange("p t j -> p (t j)"),
            )

        first = [sum(PIECES[:g]) for g in range(len(PIECES))]
        todo = [(g, k) for g in range(len(PIECES)) for k in range(PASSES + 1)]
        place = {}

        def gather(count):
            for i in range(count):
                if todo:
                    g, k = todo.pop(0)
                    n = PIECES[g] * C
                    c0 = first[g] * C // 16
                    if k < PASSES:
                        src = x_codes[k]
                        dst = slots.tile([P, 3 * C], U32, name="s_codes%d" % k, align_bytes=64)
                    else:
                        src = x_scales
                        dst = slots.tile([P, 3 * C], U8, name="s_scales", align_bytes=64)
                    nc.vector.tensor_copy(dst[:, 0:n], src[:].indirect(offs_sb[:, c0 : c0 + n // 16]))
                    for i in range(PIECES[g]):
                        place[(first[g] + i, k)] = (dst, slice(i * C, (i + 1) * C))

        parcels = [(e, None) for e in range(WHOLE)]
        for h in range(HALVES):
            parcels.extend([(e, h) for e in range(WHOLE, E)])
        raw, grouped, weights, banks = {}, {}, {}, {}
        ends = [sum(RUNS[: i + 1]) - 1 for i in range(len(RUNS))]

        def load(u):
            e, h = parcels[u]
            if h is None:
                raw[u] = raws.tile([P, PASSES, PACK, N], F32, name="w_raw")
                src = w[e].rearrange("(a p j) n -> p a (j n)", a=PASSES, j=PACK)
                nc.sync.dma_start(raw[u][:].rearrange("p a j n -> p a (j n)"), src)
            else:
                raw[u] = late.tile([P, PASSES, PACK, P], F32, name="half_raw")
                for a in range(PASSES):
                    src = w[e, a * 512 : (a + 1) * 512, h * P : (h + 1) * P].rearrange("(p j) n -> p j n", j=PACK)
                    nc.sync.dma_start(raw[u][:, a], src)

        def spread(u):
            e, h = parcels[u]
            view = raw[u][:].rearrange("p a j (c i) -> p a c j i", i=RUN)
            if h is None:
                grouped[u] = wide.tile([P, PASSES, N, PACK], BF16, name="w_grouped", align_bytes=64)
            else:
                grouped[u] = late.tile([P, PASSES, P, PACK], BF16, name="half_grouped", align_bytes=64)
            dest = grouped[u][:].rearrange("p a (c i) j -> p a c j i", i=RUN)
            if h is None and e in VECTOR_EXPERTS:
                nc.vector.tensor_copy(dest, view)
            elif h == 0:
                cut = HALF_SCALAR // RUN
                nc.scalar.copy(dest[:, :, 0:cut], view[:, :, 0:cut])
                nc.vector.tensor_copy(dest[:, :, cut:], view[:, :, cut:])
            else:
                nc.scalar.copy(dest, view)

        def quantise(u):
            e, h = parcels[u]
            n = PASSES * (N if h is None else P)
            pool, tag = (work, "w") if h is None else (late, "half")
            codes = pool.tile([P, n], U32, name=tag + "_codes", align_bytes=64)
            scales = pool.tile([P, n], U8, name=tag + "_scales", align_bytes=64)
            weights[u] = (codes, scales)
            nc.vector.quantize_mx(
                out=codes[:].bitcast(FP8X4),
                scales=scales[:],
                in_=grouped[u][:].rearrange("p a n j -> p (a n j)"),
            )

        def multiply(u):
            e, h = parcels[u]
            run = len([end for end in ends if end < u])
            u0 = ends[run] + 1 - RUNS[run]
            halves = range(HALVES) if h is None else (h,)
            if u == u0:
                for q in halves:
                    banks[(run, q)] = psum.tile([P, 4 * C], F32, name="acc%d" % q)
            w_codes, w_scales = weights[u]
            for q in halves:
                acc = banks[(run, q)]
                for a in range(PASSES):
                    c0 = a * N + q * P if h is None else a * P
                    codes, here = place[(e, a)]
                    scales, there = place[(e, PASSES)]
                    nc.tensor.matmul_mx(
                        out=acc[:, (u - u0) * C : (u - u0 + 1) * C],
                        lhsT=w_codes[:, c0 : c0 + P].bitcast(FP8X4),
                        lhsT_scale=w_scales[:, c0 : c0 + P],
                        rhs=codes[:, here].bitcast(FP8X4),
                        rhs_scale=scales[4 * a : P, there],
                        start=(a == 0),
                        stop=(a == PASSES - 1),
                    )
            if u == ends[run]:
                for q in halves:
                    for v in range(u0, u + 1):
                        f = parcels[v][0]
                        nc.scalar.activation(
                            y[q][:, f * C : (f + 1) * C],
                            banks[(run, q)][:, (v - u0) * C : (v - u0 + 1) * C],
                            SILU,
                            bias=bias[:, q, f : f + 1],
                        )

        def load_gates(h):
            for r in range(0, TOP, 2):
                nc.sync.dma_start(gates[h][:, r : r + 2, :], gate[r : r + 2, h * P : (h + 1) * P, :].rearrange("r p t -> p r t"))

        def combine(h, adds):
            low, high = slice(0, T // 2), slice(T // 2, T)
            part = prod[h]
            last = TOP - 1

            def pick(r):
                nc.vector.tensor_tensor(part[:, r, :], y[h][:].indirect(pos_sb[r][:]), gates[h][:, r, :], MULT)

            def pick_half(cols):
                offsets = pos_sb[last][:, cols.start // 16 : cols.stop // 16]
                nc.vector.tensor_tensor(part[:, last, cols], y[h][:].indirect(offsets), gates[h][:, last, cols], MULT)

            def add(r):
                nc.vector.tensor_tensor(part[:, 0, :], part[:, 0, :], part[:, r, :], ADD)

            def finish(cols):
                nc.vector.tensor_tensor(res[h][:, cols], part[:, 0, cols], part[:, last, cols], ADD)
                nc.sync.dma_start(out[h * P : (h + 1) * P, cols], res[h][:, cols])

            if h == 0:
                if not adds:
                    for r in range(TOP):
                        pick(r)
                else:
                    add(1)
                    add(2)
                    finish(slice(0, T))
            else:
                for r in range(last):
                    pick(r)
                add(1)
                pick_half(low)
                add(2)
                pick_half(high)
                finish(low)
                finish(high)

        h1 = WHOLE + LATE
        for step in range(h1 + 2):
            if step < h1:
                load(step)
            if step == 0:
                nc.sync.dma_start(bias[:], b.rearrange("(h p) e -> p h e", p=P))
            if step >= 2:
                multiply(step - 2)
            if 1 <= step <= h1:
                quantise(step - 1)
            gather(3 if step == 0 else 1)
            if step < h1:
                spread(step)
            if step == h1 - 1:
                for r, pos in enumerate((pos1, pos2, pos3, pos4)):
                    nc.sync.dma_start(pos_sb[r][:], pos)
                load_gates(0)
                for u in range(h1, len(parcels)):
                    load(u)
                load_gates(1)
        for u in range(h1, len(parcels)):
            spread(u)
        combine(0, False)
        for u in range(h1, len(parcels)):
            quantise(u)
            multiply(u)
        combine(0, True)
        combine(1, True)
